import numpy as np
import ml_dtypes


def mxq(x, axis, fmt="e4m3"):
    dtype, down = {"e4m3": (ml_dtypes.float8_e4m3fn, 7), "e5m2": (ml_dtypes.float8_e5m2, 14)}[fmt]
    v = np.moveaxis(np.asarray(x, np.float32).astype(ml_dtypes.bfloat16).astype(np.float64), axis, -1)
    blocks = v.reshape(v.shape[:-1] + (-1, 32))
    amax = np.abs(blocks).max(-1, keepdims=True)
    byte = np.maximum(np.where(amax > 0, np.frexp(amax)[1] - 1 + 127, 0) - down, 1)
    scale = np.exp2(byte - 127.0)
    codes = (blocks / scale).astype(np.float32).astype(dtype).astype(np.float64)
    return np.moveaxis((codes * scale).reshape(v.shape), -1, axis)


WIDE = False


def mx_kscale(k):
    if not WIDE:
        return np.ones(k)
    levels = np.array([10, -10, 5, -5, 0])
    if k % 512:
        return np.exp2(np.random.permutation(np.resize(levels, k // 32))).repeat(32)
    a = np.empty((k // 512, 16))
    for p in range(k // 512):
        a[p, :8] = np.random.permutation(np.resize(levels, 8))
        for g in range(8):
            far = levels[np.abs(levels - a[p, g]) >= 10]
            a[p, g + 8] = far[np.random.randint(len(far))]
    return np.exp2(a.ravel()).repeat(32)


def f64(x):
    return np.asarray(x).astype(np.float64)


def striped(idx):
    return np.tile(idx.reshape(-1, 16).T, (8, 1)).astype(np.uint16)


def unstriped(offs):
    return offs[:16].T.reshape(-1).astype(np.int64)


E2M1 = np.array([0.0, 0.5, 1.0, 1.5, 2.0, 3.0, 4.0, 6.0, -0.0, -0.5, -1.0, -1.5, -2.0, -3.0, -4.0, -6.0])


def pack_weight(w, fmt):
    k, n = w.shape
    w = f64(np.asarray(w, np.float32).astype(ml_dtypes.bfloat16)).reshape(k // 32, 32, n)
    amax = np.abs(w).max(1)
    if fmt == "e4m3":
        byte = np.frexp(amax)[1] - 1 + 127 - 7
    else:
        mant, ex = np.frexp(amax / 6.0)
        byte = np.where(mant > 0.5, ex, ex - 1) + 127
    byte = np.clip(np.where(amax > 0, byte, 1), 1, 254)
    scaled = (w * np.exp2(127.0 - byte)[:, None, :]).reshape(k, n).astype(np.float32)
    by_word = np.ascontiguousarray(scaled.reshape(k // 512, 128, 4, n).transpose(0, 1, 3, 2))
    if fmt == "e4m3":
        words = by_word.astype(ml_dtypes.float8_e4m3fn).view(np.uint8)
    else:
        c = by_word.astype(ml_dtypes.float4_e2m1fn).view(np.uint8) & 0xF
        words = (c[..., 0::2] | (c[..., 1::2] << 4)).reshape(k // 512, 128, 2 * n)
    return np.ascontiguousarray(words), np.ascontiguousarray(byte.astype(np.uint8).reshape(k // 512, 16, n))


def unpack_weight(words, scales, fmt):
    g, _, n = scales.shape
    words = np.ascontiguousarray(words).reshape(g, 128, n, -1)
    if fmt == "e4m3":
        vals = words.view(ml_dtypes.float8_e4m3fn).astype(np.float64)
    else:
        nib = np.empty((g, 128, n, 4), np.uint8)
        nib[..., 0::2] = words & 0xF
        nib[..., 1::2] = words >> 4
        vals = E2M1[nib]
    vals = vals * np.repeat(np.exp2(scales.astype(np.float64) - 127.0), 8, axis=1)[..., None]
    return vals.transpose(0, 1, 3, 2).reshape(g * 512, n)


def relu2(v):
    return np.maximum(v, 0.0) ** 2


K, T, E, C, H, N = 512, 768, 4, 128, 512, 128


def by_expert(wq, xq):
    return np.concatenate([wq[e].T @ xq[:, e * C:(e + 1) * C] for e in range(E)], axis=1)


def setup_inputs():
    n = np.random.standard_normal
    s = mx_kscale(K)[:, None]
    u = mx_kscale(H)
    w1 = [pack_weight(m, "e2m1") for m in n((E, K, H)) / np.sqrt(K) / s[None] * u[None, None, :]]
    w2 = [pack_weight(m, "e2m1") for m in n((E, H, N)) / np.sqrt(H) / u[None, :, None] ** 2]
    return {
        "xT": (n((K, T)) * s).astype(np.float32),
        "xr": n((N, T)).astype(np.float32),
        "w1_words": np.stack([m[0] for m in w1]),
        "w1_scales": np.stack([m[1] for m in w1]),
        "w2_words": np.stack([m[0] for m in w2]),
        "w2_scales": np.stack([m[1] for m in w2]),
        "gate": np.tile(np.random.uniform(0.2, 1.0, E * C), (N, 1)).astype(np.float32),
        "offs": striped(np.random.permutation(T)[:E * C]),
    }


def reference(xT, xr, w1_words, w1_scales, w2_words, w2_scales, gate, offs):
    idx = unstriped(offs)
    w1 = np.stack([unpack_weight(w1_words[e], w1_scales[e], "e2m1") for e in range(E)])
    w2 = np.stack([unpack_weight(w2_words[e], w2_scales[e], "e2m1") for e in range(E)])
    xq = mxq(f64(xT)[:, idx], 0, "e4m3")
    h = relu2(by_expert(w1, xq))
    y = by_expert(w2, mxq(h, 0, "e4m3"))
    out = f64(xr).copy()
    out[:, idx] += f64(gate) * y
    return out

@@ -1,0 +1,259 @@
+from contextlib import ExitStack
+
+import concourse.mybir as mybir
+
+F32 = mybir.dt.float32
+BF16 = mybir.dt.bfloat16
+I32 = mybir.dt.int32
+U32 = mybir.dt.uint32
+U16 = mybir.dt.uint16
+U8 = mybir.dt.uint8
+FP8X4 = mybir.dt.float8_e4m3fn_x4
+FP4X4 = mybir.dt.float4_e2m1fn_x4
+ACT = mybir.ActivationFunctionType
+ALU = mybir.AluOpType
+
+P = 128
+PACK = 4
+K, T, E, C, H, N = 512, 768, 4, 128, 512, 128
+S = E * C
+
+FLOPS = 2 * S * (K * H + H * N)
+
+
+def tile_moe_res_mlp_relu2_kernel(
+    tc, xT, xr, w1_words, w1_scales, w2_words, w2_scales, gate, offs, out
+):
+    nc = tc.nc
+    with ExitStack() as ctx:
+        keep = ctx.enter_context(tc.tile_pool(name="keep", bufs=1))
+        work = ctx.enter_context(tc.tile_pool(name="work", bufs=4))
+        psum = ctx.enter_context(tc.psum_pool(name="psum", bufs=4))
+
+        offsets = keep.tile([P, S // 16], U16, name="offsets")
+        w1_raw = keep.tile([P, E * 2 * H], U8, align_bytes=64, name="w1_raw")
+        w1_perm = keep.tile([P, E * 2 * H], U8, align_bytes=64, name="w1_perm")
+        s1_raw = keep.tile([P, E * H], U8, align_bytes=64, name="s1_raw")
+        s1_perm = keep.tile([P, E * H], U8, align_bytes=64, name="s1_perm")
+        w2_sb = keep.tile([P, E * 2 * N], U8, align_bytes=64, name="w2_sb")
+        s2_sb = keep.tile([P, E * N], U8, align_bytes=64, name="s2_sb")
+        tok_words = keep.tile([P, T], U32, align_bytes=64, name="tok_words")
+        tok_scales = keep.tile([P, T], U8, align_bytes=64, name="tok_scales")
+        slot_words = keep.tile([P, S], U32, align_bytes=64, name="slot_words")
+        slot_scales = keep.tile([P, S], U8, align_bytes=64, name="slot_scales")
+        window = keep.tile([P, T], F32, name="window")
+        xr_sb = keep.tile([P, T], F32, name="xr_sb")
+        gate_sb = keep.tile([P, S], F32, name="gate_sb")
+        out_sb = keep.tile([P, T], F32, name="out_sb")
+        dummy = keep.tile([P, 2], F32, name="dummy")
+
+        nc.gpsimd.memset(s1_raw[:].bitcast(I32), 0)
+        nc.gpsimd.memset(dummy[:, 0:1], 0.0)
+        nc.gpsimd.memset(s2_sb[:].bitcast(I32), 0)
+        nc.gpsimd.memset(tok_scales[:], 0)
+        nc.gpsimd.memset(window[:], 0.0)
+        nc.scalar.activation(out=dummy[:, 1:2], in_=dummy[:, 0:1], func=ACT.Relu)
+        nc.sync.dma_start(
+            out=w1_raw[:].bitcast(I32).rearrange("p (e b) -> p e b", e=E)[:, 0:2, :],
+            in_=w1_words.bitcast(I32).rearrange("e s p b -> p (e s) b")[:, 0:2, :],
+        )
+        raw0 = keep.tile([P, PACK, 256], F32, name="raw0")
+        nc.sync.dma_start(out=raw0[:], in_=xT.rearrange("(p j) t -> p j t", j=PACK)[:, :, 0:256])
+        for q in range(4):
+            nc.scalar.dma_start(
+                out=s1_raw[32 * q : 32 * q + 4, :].bitcast(I32).rearrange("r (e b) -> r e b", e=E),
+                in_=w1_scales.bitcast(I32).rearrange("e s r b -> r (e s) b")[4 * q : 4 * q + 4, :, :],
+            )
+        raw1 = keep.tile([P, PACK, 256], F32, name="raw1")
+        nc.sync.dma_start(out=raw1[:], in_=xT.rearrange("(p j) t -> p j t", j=PACK)[:, :, 256:512])
+        raw2 = keep.tile([P, PACK, 256], F32, name="raw2")
+        nc.sync.dma_start(out=raw2[:], in_=xT.rearrange("(p j) t -> p j t", j=PACK)[:, :, 512:768])
+        nc.sync.dma_start(offsets[:], offs)
+        nc.sync.dma_start(
+            out=w1_raw[:].bitcast(I32).rearrange("p (e b) -> p e b", e=E)[:, 2:4, :],
+            in_=w1_words.bitcast(I32).rearrange("e s p b -> p (e s) b")[:, 2:4, :],
+        )
+        nc.sync.dma_start(
+            out=w2_sb[:].bitcast(I32).rearrange("p (e b) -> p e b", e=E),
+            in_=w2_words.bitcast(I32).rearrange("e s p b -> p (e s) b"),
+        )
+        for q in range(4):
+            nc.sync.dma_start(
+                out=s2_sb[32 * q : 32 * q + 4, :].bitcast(I32).rearrange("r (e b) -> r e b", e=E),
+                in_=w2_scales.bitcast(I32).rearrange("e s r b -> r (e s) b")[4 * q : 4 * q + 4, :, :],
+            )
+        nc.sync.dma_start(out=gate_sb[:], in_=gate)
+        nc.sync.dma_start(out=xr_sb[:], in_=xr)
+        nc.vector.tensor_copy(
+            out=s1_perm[:, 0 * H : 4 * H].rearrange("p (e t m) -> p e t m", e=4, t=PACK),
+            in_=s1_raw[:, 0 * H : 4 * H].rearrange("p (e m t) -> p e t m", e=4, t=PACK),
+        )
+        nc.vector.tensor_copy(
+            out=w1_perm[:].bitcast(U16)[:, 0 * H : 2 * H].rearrange("p (e t m) -> p e t m", e=2, t=PACK),
+            in_=w1_raw[:].bitcast(U16)[:, 0 * H : 2 * H].rearrange("p (e m t) -> p e t m", e=2, t=PACK),
+        )
+        grouped0 = keep.tile([P, 256, PACK], BF16, align_bytes=64, name="grouped0")
+        nc.scalar.copy(out=grouped0[:, :256, :], in_=raw0[:, :, :256].rearrange("p j t -> p t j"))
+        nc.vector.quantize_mx(
+            out=tok_words[:, 0:256].bitcast(FP8X4),
+            scales=tok_scales[:, 0:256],
+            in_=grouped0[:].rearrange("p t j -> p (t j)"),
+        )
+        grouped1 = keep.tile([P, 256, PACK], BF16, align_bytes=64, name="grouped1")
+        nc.scalar.copy(out=grouped1[:, :176, :], in_=raw1[:, :, :176].rearrange("p j t -> p t j"))
+        nc.vector.tensor_copy(out=grouped1[:, 176:, :], in_=raw1[:, :, 176:].rearrange("p j t -> p t j"))
+        nc.vector.quantize_mx(
+            out=tok_words[:, 256:512].bitcast(FP8X4),
+            scales=tok_scales[:, 256:512],
+            in_=grouped1[:].rearrange("p t j -> p (t j)"),
+        )
+        grouped2 = keep.tile([P, 256, PACK], BF16, align_bytes=64, name="grouped2")
+        nc.scalar.copy(out=grouped2[:, :96, :], in_=raw2[:, :, :96].rearrange("p j t -> p t j"))
+        nc.vector.tensor_copy(out=grouped2[:, 96:, :], in_=raw2[:, :, 96:].rearrange("p j t -> p t j"))
+        nc.vector.quantize_mx(
+            out=tok_words[:, 512:768].bitcast(FP8X4),
+            scales=tok_scales[:, 512:768],
+            in_=grouped2[:].rearrange("p t j -> p (t j)"),
+        )
+        nc.vector.tensor_copy(out=slot_words[:, 0:128], in_=tok_words[:].indirect(offsets[:, 0:8]))
+        nc.vector.tensor_copy(out=slot_scales[:, 0:128], in_=tok_scales[:].indirect(offsets[:, 0:8]))
+        nc.vector.tensor_copy(out=slot_words[:, 128:256], in_=tok_words[:].indirect(offsets[:, 8:16]))
+        nc.vector.tensor_copy(out=slot_scales[:, 128:256], in_=tok_scales[:].indirect(offsets[:, 8:16]))
+        nc.vector.tensor_copy(
+            out=w1_perm[:].bitcast(U16)[:, 2 * H : 4 * H].rearrange("p (e t m) -> p e t m", e=2, t=PACK),
+            in_=w1_raw[:].bitcast(U16)[:, 2 * H : 4 * H].rearrange("p (e m t) -> p e t m", e=2, t=PACK),
+        )
+        nc.vector.tensor_copy(out=slot_words[:, 256:512], in_=tok_words[:].indirect(offsets[:, 16:32]))
+        nc.vector.tensor_copy(out=slot_scales[:, 256:512], in_=tok_scales[:].indirect(offsets[:, 16:32]))
+        a_ps0 = psum.tile([P, PACK, C], F32, tag="a_ps", name="a_ps0")
+        for t in range(PACK):
+            b = 0 * H + t * P
+            nc.tensor.matmul_mx(
+                out=a_ps0[:, t, :],
+                lhsT=w1_perm[:, 2 * b : 2 * b + 2 * P].bitcast(FP4X4),
+                lhsT_scale=s1_perm[:, b : b + P],
+                rhs=slot_words[:, 0:128].bitcast(FP8X4),
+                rhs_scale=slot_scales[:, 0:128],
+                start=True,
+                stop=True,
+            )
+        r0 = work.tile([P, C, PACK], F32, tag="r", name="r0")
+        nc.scalar.activation(out=r0[:], in_=a_ps0[:].rearrange("p t c -> p c t"), func=ACT.Relu)
+        hb0 = work.tile([P, C * PACK], BF16, align_bytes=64, tag="hb", name="hb0")
+        nc.scalar.activation(out=hb0[:], in_=r0[:].rearrange("p c t -> p (c t)"), func=ACT.Square)
+        a_ps1 = psum.tile([P, PACK, C], F32, tag="a_ps", name="a_ps1")
+        for t in range(PACK):
+            b = 1 * H + t * P
+            nc.tensor.matmul_mx(
+                out=a_ps1[:, t, :],
+                lhsT=w1_perm[:, 2 * b : 2 * b + 2 * P].bitcast(FP4X4),
+                lhsT_scale=s1_perm[:, b : b + P],
+                rhs=slot_words[:, 128:256].bitcast(FP8X4),
+                rhs_scale=slot_scales[:, 128:256],
+                start=True,
+                stop=True,
+            )
+        r1 = work.tile([P, C, PACK], F32, tag="r", name="r1")
+        nc.scalar.activation(out=r1[:], in_=a_ps1[:].rearrange("p t c -> p c t"), func=ACT.Relu)
+        h_words0 = work.tile([P, C], U32, align_bytes=64, tag="h_words", name="h_words0")
+        h_scales0 = work.tile([P, C], U8, align_bytes=64, tag="h_scales", name="h_scales0")
+        nc.vector.quantize_mx(out=h_words0[:].bitcast(FP8X4), scales=h_scales0[:], in_=hb0[:])
+        hb1 = work.tile([P, C * PACK], BF16, align_bytes=64, tag="hb", name="hb1")
+        nc.scalar.activation(out=hb1[:], in_=r1[:].rearrange("p c t -> p (c t)"), func=ACT.Square)
+        y_ps0 = psum.tile([P, C], F32, tag="y_ps", name="y_ps0")
+        nc.tensor.matmul_mx(
+            out=y_ps0[:],
+            lhsT=w2_sb[:, 0 * 2 * N : 1 * 2 * N].bitcast(FP4X4),
+            lhsT_scale=s2_sb[:, 0 * N : 1 * N],
+            rhs=h_words0[:].bitcast(FP8X4),
+            rhs_scale=h_scales0[:],
+            start=True,
+            stop=True,
+        )
+        a_ps2 = psum.tile([P, PACK, C], F32, tag="a_ps", name="a_ps2")
+        for t in range(PACK):
+            b = 2 * H + t * P
+            nc.tensor.matmul_mx(
+                out=a_ps2[:, t, :],
+                lhsT=w1_perm[:, 2 * b : 2 * b + 2 * P].bitcast(FP4X4),
+                lhsT_scale=s1_perm[:, b : b + P],
+                rhs=slot_words[:, 256:384].bitcast(FP8X4),
+                rhs_scale=slot_scales[:, 256:384],
+                start=True,
+                stop=True,
+            )
+        r2 = work.tile([P, C, PACK], F32, tag="r", name="r2")
+        nc.scalar.activation(out=r2[:], in_=a_ps2[:].rearrange("p t c -> p c t"), func=ACT.Relu)
+        h_words1 = work.tile([P, C], U32, align_bytes=64, tag="h_words", name="h_words1")
+        h_scales1 = work.tile([P, C], U8, align_bytes=64, tag="h_scales", name="h_scales1")
+        nc.vector.quantize_mx(out=h_words1[:].bitcast(FP8X4), scales=h_scales1[:], in_=hb1[:])
+        y_sb0 = work.tile([P, C], F32, tag="y_sb", name="y_sb0")
+        nc.scalar.copy(out=y_sb0[:], in_=y_ps0[:])
+        a_ps3 = psum.tile([P, PACK, C], F32, tag="a_ps", name="a_ps3")
+        for t in range(PACK):
+            b = 3 * H + t * P
+            nc.tensor.matmul_mx(
+                out=a_ps3[:, t, :],
+                lhsT=w1_perm[:, 2 * b : 2 * b + 2 * P].bitcast(FP4X4),
+                lhsT_scale=s1_perm[:, b : b + P],
+                rhs=slot_words[:, 384:512].bitcast(FP8X4),
+                rhs_scale=slot_scales[:, 384:512],
+                start=True,
+                stop=True,
+            )
+        r3 = work.tile([P, C, PACK], F32, tag="r", name="r3")
+        nc.scalar.activation(out=r3[:], in_=a_ps3[:].rearrange("p t c -> p c t"), func=ACT.Relu)
+        y_ps1 = psum.tile([P, C], F32, tag="y_ps", name="y_ps1")
+        nc.tensor.matmul_mx(
+            out=y_ps1[:],
+            lhsT=w2_sb[:, 1 * 2 * N : 2 * 2 * N].bitcast(FP4X4),
+            lhsT_scale=s2_sb[:, 1 * N : 2 * N],
+            rhs=h_words1[:].bitcast(FP8X4),
+            rhs_scale=h_scales1[:],
+            start=True,
+            stop=True,
+        )
+        nc.vector.tensor_tensor(window[:].indirect(offsets[:, 0:8]), y_sb0[:], gate_sb[:, 0:128], ALU.mult)
+        hb2 = work.tile([P, C * PACK], BF16, align_bytes=64, tag="hb", name="hb2")
+        nc.scalar.activation(out=hb2[:], in_=r2[:].rearrange("p c t -> p (c t)"), func=ACT.Square)
+        y_sb1 = work.tile([P, C], F32, tag="y_sb", name="y_sb1")
+        nc.scalar.copy(out=y_sb1[:], in_=y_ps1[:])
+        h_words2 = work.tile([P, C], U32, align_bytes=64, tag="h_words", name="h_words2")
+        h_scales2 = work.tile([P, C], U8, align_bytes=64, tag="h_scales", name="h_scales2")
+        nc.vector.quantize_mx(out=h_words2[:].bitcast(FP8X4), scales=h_scales2[:], in_=hb2[:])
+        nc.vector.tensor_tensor(window[:].indirect(offsets[:, 8:16]), y_sb1[:], gate_sb[:, 128:256], ALU.mult)
+        hb3 = work.tile([P, C * PACK], BF16, align_bytes=64, tag="hb", name="hb3")
+        nc.scalar.activation(out=hb3[:], in_=r3[:].rearrange("p c t -> p (c t)"), func=ACT.Square)
+        y_ps2 = psum.tile([P, C], F32, tag="y_ps", name="y_ps2")
+        nc.tensor.matmul_mx(
+            out=y_ps2[:],
+            lhsT=w2_sb[:, 2 * 2 * N : 3 * 2 * N].bitcast(FP4X4),
+            lhsT_scale=s2_sb[:, 2 * N : 3 * N],
+            rhs=h_words2[:].bitcast(FP8X4),
+            rhs_scale=h_scales2[:],
+            start=True,
+            stop=True,
+        )
+        y_sb2 = work.tile([P, C], F32, tag="y_sb", name="y_sb2")
+        nc.scalar.copy(out=y_sb2[:], in_=y_ps2[:])
+        h_words3 = work.tile([P, C], U32, align_bytes=64, tag="h_words", name="h_words3")
+        h_scales3 = work.tile([P, C], U8, align_bytes=64, tag="h_scales", name="h_scales3")
+        nc.vector.quantize_mx(out=h_words3[:].bitcast(FP8X4), scales=h_scales3[:], in_=hb3[:])
+        nc.vector.tensor_tensor(window[:].indirect(offsets[:, 16:24]), y_sb2[:], gate_sb[:, 256:384], ALU.mult)
+        y_ps3 = psum.tile([P, C], F32, tag="y_ps", name="y_ps3")
+        nc.tensor.matmul_mx(
+            out=y_ps3[:],
+            lhsT=w2_sb[:, 3 * 2 * N : 4 * 2 * N].bitcast(FP4X4),
+            lhsT_scale=s2_sb[:, 3 * N : 4 * N],
+            rhs=h_words3[:].bitcast(FP8X4),
+            rhs_scale=h_scales3[:],
+            start=True,
+            stop=True,
+        )
+        y_sb3 = work.tile([P, C], F32, tag="y_sb", name="y_sb3")
+        nc.scalar.copy(out=y_sb3[:], in_=y_ps3[:])
+        nc.vector.tensor_tensor(window[:].indirect(offsets[:, 24:32]), y_sb3[:], gate_sb[:, 384:512], ALU.mult)
+        nc.vector.tensor_tensor(out_sb[:, 0:384], window[:, 0:384], xr_sb[:, 0:384], ALU.add)
+        nc.sync.dma_start(out=out[:, 0:384], in_=out_sb[:, 0:384])
+        nc.vector.tensor_tensor(out_sb[:, 384:768], window[:, 384:768], xr_sb[:, 384:768], ALU.add)
+        nc.sync.dma_start(out=out[:, 384:768], in_=out_sb[:, 384:768])

@@ -1,6 +1,7 @@
 from contextlib import ExitStack
 
 import concourse.mybir as mybir
+from concourse.masks import make_identity
 
 F32 = mybir.dt.float32
 BF16 = mybir.dt.bfloat16
@@ -28,13 +29,13 @@ def tile_moe_res_mlp_relu2_kernel(
     with ExitStack() as ctx:
         keep = ctx.enter_context(tc.tile_pool(name="keep", bufs=1))
         work = ctx.enter_context(tc.tile_pool(name="work", bufs=4))
-        psum = ctx.enter_context(tc.psum_pool(name="psum", bufs=4))
+        psum = ctx.enter_context(tc.psum_pool(name="psum", bufs=1))
 
         offsets = keep.tile([P, S // 16], U16, name="offsets")
         w1_raw = keep.tile([P, E * 2 * H], U8, align_bytes=64, name="w1_raw")
-        w1_perm = keep.tile([P, E * 2 * H], U8, align_bytes=64, name="w1_perm")
         s1_raw = keep.tile([P, E * H], U8, align_bytes=64, name="s1_raw")
-        s1_perm = keep.tile([P, E * H], U8, align_bytes=64, name="s1_perm")
+        w1_perm = keep.tile([P, 1 * 2 * H], U8, align_bytes=64, name="w1_perm")
+        s1_perm = keep.tile([P, 1 * H], U8, align_bytes=64, name="s1_perm")
         w2_sb = keep.tile([P, E * 2 * N], U8, align_bytes=64, name="w2_sb")
         s2_sb = keep.tile([P, E * N], U8, align_bytes=64, name="s2_sb")
         tok_words = keep.tile([P, T], U32, align_bytes=64, name="tok_words")
@@ -45,33 +46,35 @@ def tile_moe_res_mlp_relu2_kernel(
         xr_sb = keep.tile([P, T], F32, name="xr_sb")
         gate_sb = keep.tile([P, S], F32, name="gate_sb")
         out_sb = keep.tile([P, T], F32, name="out_sb")
+        ident = keep.tile([P, P], F32, name="ident")
         dummy = keep.tile([P, 2], F32, name="dummy")
 
         nc.gpsimd.memset(s1_raw[:].bitcast(I32), 0)
         nc.gpsimd.memset(dummy[:, 0:1], 0.0)
         nc.gpsimd.memset(s2_sb[:].bitcast(I32), 0)
         nc.gpsimd.memset(tok_scales[:], 0)
+        make_identity(nc, ident[:])
         nc.gpsimd.memset(window[:], 0.0)
         nc.scalar.activation(out=dummy[:, 1:2], in_=dummy[:, 0:1], func=ACT.Relu)
         nc.sync.dma_start(
-            out=w1_raw[:].bitcast(I32).rearrange("p (e b) -> p e b", e=E)[:, 0:2, :],
-            in_=w1_words.bitcast(I32).rearrange("e s p b -> p (e s) b")[:, 0:2, :],
+            out=w1_raw[:].bitcast(I32).rearrange("p (e b) -> p e b", e=E)[:, 0:1, :],
+            in_=w1_words.bitcast(I32).rearrange("e s p b -> p (e s) b")[:, 0:1, :],
         )
         raw0 = keep.tile([P, PACK, 256], F32, name="raw0")
         nc.sync.dma_start(out=raw0[:], in_=xT.rearrange("(p j) t -> p j t", j=PACK)[:, :, 0:256])
         for q in range(4):
-            nc.scalar.dma_start(
+            nc.sync.dma_start(
                 out=s1_raw[32 * q : 32 * q + 4, :].bitcast(I32).rearrange("r (e b) -> r e b", e=E),
                 in_=w1_scales.bitcast(I32).rearrange("e s r b -> r (e s) b")[4 * q : 4 * q + 4, :, :],
             )
         raw1 = keep.tile([P, PACK, 256], F32, name="raw1")
         nc.sync.dma_start(out=raw1[:], in_=xT.rearrange("(p j) t -> p j t", j=PACK)[:, :, 256:512])
+        nc.sync.dma_start(offsets[:], offs)
         raw2 = keep.tile([P, PACK, 256], F32, name="raw2")
         nc.sync.dma_start(out=raw2[:], in_=xT.rearrange("(p j) t -> p j t", j=PACK)[:, :, 512:768])
-        nc.sync.dma_start(offsets[:], offs)
         nc.sync.dma_start(
-            out=w1_raw[:].bitcast(I32).rearrange("p (e b) -> p e b", e=E)[:, 2:4, :],
-            in_=w1_words.bitcast(I32).rearrange("e s p b -> p (e s) b")[:, 2:4, :],
+            out=w1_raw[:].bitcast(I32).rearrange("p (e b) -> p e b", e=E)[:, 1:4, :],
+            in_=w1_words.bitcast(I32).rearrange("e s p b -> p (e s) b")[:, 1:4, :],
         )
         nc.sync.dma_start(
             out=w2_sb[:].bitcast(I32).rearrange("p (e b) -> p e b", e=E),
@@ -85,47 +88,46 @@ def tile_moe_res_mlp_relu2_kernel(
         nc.sync.dma_start(out=gate_sb[:], in_=gate)
         nc.sync.dma_start(out=xr_sb[:], in_=xr)
         nc.vector.tensor_copy(
-            out=s1_perm[:, 0 * H : 4 * H].rearrange("p (e t m) -> p e t m", e=4, t=PACK),
-            in_=s1_raw[:, 0 * H : 4 * H].rearrange("p (e m t) -> p e t m", e=4, t=PACK),
+            out=w1_perm[:].bitcast(U16)[:, 0 * H : 1 * H].rearrange("p (t m) -> p t m", t=PACK),
+            in_=w1_raw[:].bitcast(U16)[:, 0 * H : 1 * H].rearrange("p (m t) -> p t m", t=PACK),
         )
         nc.vector.tensor_copy(
-            out=w1_perm[:].bitcast(U16)[:, 0 * H : 2 * H].rearrange("p (e t m) -> p e t m", e=2, t=PACK),
-            in_=w1_raw[:].bitcast(U16)[:, 0 * H : 2 * H].rearrange("p (e m t) -> p e t m", e=2, t=PACK),
+            out=s1_perm[:, 0 * H : 1 * H].rearrange("p (t m) -> p t m", t=PACK),
+            in_=s1_raw[:, 0 * H : 1 * H].rearrange("p (m t) -> p t m", t=PACK),
         )
         grouped0 = keep.tile([P, 256, PACK], BF16, align_bytes=64, name="grouped0")
-        nc.scalar.copy(out=grouped0[:, :256, :], in_=raw0[:, :, :256].rearrange("p j t -> p t j"))
+        nc.scalar.copy(out=grouped0[:, 0:160, :].rearrange("p (c i) j -> p c j i", i=4), in_=raw0[:, :, 0:160].rearrange("p j (c i) -> p c j i", i=4))
+        nc.vector.tensor_copy(out=grouped0[:, 160:256, :].rearrange("p (c i) j -> p c j i", i=4), in_=raw0[:, :, 160:256].rearrange("p j (c i) -> p c j i", i=4))
         nc.vector.quantize_mx(
             out=tok_words[:, 0:256].bitcast(FP8X4),
             scales=tok_scales[:, 0:256],
-            in_=grouped0[:].rearrange("p t j -> p (t j)"),
+            in_=grouped0[:, 0:256, :].rearrange("p t j -> p (t j)"),
         )
         grouped1 = keep.tile([P, 256, PACK], BF16, align_bytes=64, name="grouped1")
-        nc.scalar.copy(out=grouped1[:, :176, :], in_=raw1[:, :, :176].rearrange("p j t -> p t j"))
-        nc.vector.tensor_copy(out=grouped1[:, 176:, :], in_=raw1[:, :, 176:].rearrange("p j t -> p t j"))
+        nc.scalar.copy(out=grouped1[:, 0:144, :].rearrange("p (c i) j -> p c j i", i=4), in_=raw1[:, :, 0:144].rearrange("p j (c i) -> p c j i", i=4))
+        nc.vector.tensor_copy(out=grouped1[:, 144:256, :].rearrange("p (c i) j -> p c j i", i=4), in_=raw1[:, :, 144:256].rearrange("p j (c i) -> p c j i", i=4))
         nc.vector.quantize_mx(
             out=tok_words[:, 256:512].bitcast(FP8X4),
             scales=tok_scales[:, 256:512],
-            in_=grouped1[:].rearrange("p t j -> p (t j)"),
+            in_=grouped1[:, 0:256, :].rearrange("p t j -> p (t j)"),
         )
         grouped2 = keep.tile([P, 256, PACK], BF16, align_bytes=64, name="grouped2")
-        nc.scalar.copy(out=grouped2[:, :96, :], in_=raw2[:, :, :96].rearrange("p j t -> p t j"))
-        nc.vector.tensor_copy(out=grouped2[:, 96:, :], in_=raw2[:, :, 96:].rearrange("p j t -> p t j"))
+        nc.scalar.copy(out=grouped2[:, 0:80, :].rearrange("p (c i) j -> p c j i", i=4), in_=raw2[:, :, 0:80].rearrange("p j (c i) -> p c j i", i=4))
+        nc.vector.tensor_copy(out=grouped2[:, 80:256, :].rearrange("p (c i) j -> p c j i", i=4), in_=raw2[:, :, 80:256].rearrange("p j (c i) -> p c j i", i=4))
         nc.vector.quantize_mx(
             out=tok_words[:, 512:768].bitcast(FP8X4),
             scales=tok_scales[:, 512:768],
-            in_=grouped2[:].rearrange("p t j -> p (t j)"),
+            in_=grouped2[:, 0:256, :].rearrange("p t j -> p (t j)"),
         )
         nc.vector.tensor_copy(out=slot_words[:, 0:128], in_=tok_words[:].indirect(offsets[:, 0:8]))
         nc.vector.tensor_copy(out=slot_scales[:, 0:128], in_=tok_scales[:].indirect(offsets[:, 0:8]))
         nc.vector.tensor_copy(out=slot_words[:, 128:256], in_=tok_words[:].indirect(offsets[:, 8:16]))
         nc.vector.tensor_copy(out=slot_scales[:, 128:256], in_=tok_scales[:].indirect(offsets[:, 8:16]))
-        nc.vector.tensor_copy(
-            out=w1_perm[:].bitcast(U16)[:, 2 * H : 4 * H].rearrange("p (e t m) -> p e t m", e=2, t=PACK),
-            in_=w1_raw[:].bitcast(U16)[:, 2 * H : 4 * H].rearrange("p (e m t) -> p e t m", e=2, t=PACK),
-        )
-        nc.vector.tensor_copy(out=slot_words[:, 256:512], in_=tok_words[:].indirect(offsets[:, 16:32]))
-        nc.vector.tensor_copy(out=slot_scales[:, 256:512], in_=tok_scales[:].indirect(offsets[:, 16:32]))
-        a_ps0 = psum.tile([P, PACK, C], F32, tag="a_ps", name="a_ps0")
+        nc.vector.tensor_copy(out=slot_words[:, 256:384], in_=tok_words[:].indirect(offsets[:, 16:24]))
+        nc.vector.tensor_copy(out=slot_scales[:, 256:384], in_=tok_scales[:].indirect(offsets[:, 16:24]))
+        nc.vector.tensor_copy(out=slot_words[:, 384:512], in_=tok_words[:].indirect(offsets[:, 24:32]))
+        nc.vector.tensor_copy(out=slot_scales[:, 384:512], in_=tok_scales[:].indirect(offsets[:, 24:32]))
+        a_ps0 = psum.tile([P, PACK, C], F32, tag="a_ps", bufs=3, name="a_ps0")
         for t in range(PACK):
             b = 0 * H + t * P
             nc.tensor.matmul_mx(
@@ -139,28 +141,12 @@ def tile_moe_res_mlp_relu2_kernel(
             )
         r0 = work.tile([P, C, PACK], F32, tag="r", name="r0")
         nc.scalar.activation(out=r0[:], in_=a_ps0[:].rearrange("p t c -> p c t"), func=ACT.Relu)
-        hb0 = work.tile([P, C * PACK], BF16, align_bytes=64, tag="hb", name="hb0")
-        nc.scalar.activation(out=hb0[:], in_=r0[:].rearrange("p c t -> p (c t)"), func=ACT.Square)
-        a_ps1 = psum.tile([P, PACK, C], F32, tag="a_ps", name="a_ps1")
-        for t in range(PACK):
-            b = 1 * H + t * P
-            nc.tensor.matmul_mx(
-                out=a_ps1[:, t, :],
-                lhsT=w1_perm[:, 2 * b : 2 * b + 2 * P].bitcast(FP4X4),
-                lhsT_scale=s1_perm[:, b : b + P],
-                rhs=slot_words[:, 128:256].bitcast(FP8X4),
-                rhs_scale=slot_scales[:, 128:256],
-                start=True,
-                stop=True,
-            )
-        r1 = work.tile([P, C, PACK], F32, tag="r", name="r1")
-        nc.scalar.activation(out=r1[:], in_=a_ps1[:].rearrange("p t c -> p c t"), func=ACT.Relu)
+        hb0 = work.tile([P, C, PACK], BF16, align_bytes=64, tag="hb", name="hb0")
+        nc.scalar.activation(out=hb0[:], in_=r0[:], func=ACT.Square)
         h_words0 = work.tile([P, C], U32, align_bytes=64, tag="h_words", name="h_words0")
         h_scales0 = work.tile([P, C], U8, align_bytes=64, tag="h_scales", name="h_scales0")
-        nc.vector.quantize_mx(out=h_words0[:].bitcast(FP8X4), scales=h_scales0[:], in_=hb0[:])
-        hb1 = work.tile([P, C * PACK], BF16, align_bytes=64, tag="hb", name="hb1")
-        nc.scalar.activation(out=hb1[:], in_=r1[:].rearrange("p c t -> p (c t)"), func=ACT.Square)
-        y_ps0 = psum.tile([P, C], F32, tag="y_ps", name="y_ps0")
+        nc.vector.quantize_mx(out=h_words0[:].bitcast(FP8X4), scales=h_scales0[:], in_=hb0[:].rearrange("p c t -> p (c t)"))
+        y_ps0 = psum.tile([P, C], F32, tag="y_ps", bufs=3, name="y_ps0")
         nc.tensor.matmul_mx(
             out=y_ps0[:],
             lhsT=w2_sb[:, 0 * 2 * N : 1 * 2 * N].bitcast(FP4X4),
@@ -170,40 +156,30 @@ def tile_moe_res_mlp_relu2_kernel(
             start=True,
             stop=True,
         )
-        a_ps2 = psum.tile([P, PACK, C], F32, tag="a_ps", name="a_ps2")
-        for t in range(PACK):
-            b = 2 * H + t * P
-            nc.tensor.matmul_mx(
-                out=a_ps2[:, t, :],
-                lhsT=w1_perm[:, 2 * b : 2 * b + 2 * P].bitcast(FP4X4),
-                lhsT_scale=s1_perm[:, b : b + P],
-                rhs=slot_words[:, 256:384].bitcast(FP8X4),
-                rhs_scale=slot_scales[:, 256:384],
-                start=True,
-                stop=True,
-            )
-        r2 = work.tile([P, C, PACK], F32, tag="r", name="r2")
-        nc.scalar.activation(out=r2[:], in_=a_ps2[:].rearrange("p t c -> p c t"), func=ACT.Relu)
-        h_words1 = work.tile([P, C], U32, align_bytes=64, tag="h_words", name="h_words1")
-        h_scales1 = work.tile([P, C], U8, align_bytes=64, tag="h_scales", name="h_scales1")
-        nc.vector.quantize_mx(out=h_words1[:].bitcast(FP8X4), scales=h_scales1[:], in_=hb1[:])
         y_sb0 = work.tile([P, C], F32, tag="y_sb", name="y_sb0")
         nc.scalar.copy(out=y_sb0[:], in_=y_ps0[:])
-        a_ps3 = psum.tile([P, PACK, C], F32, tag="a_ps", name="a_ps3")
+        nc.vector.tensor_tensor(window[:].indirect(offsets[:, 0:8]), y_sb0[:], gate_sb[:, 0:128], ALU.mult)
+        a_ps1 = psum.tile([P, H], F32, tag="a_ps", bufs=3, name="a_ps1")
+        nc.tensor.matmul_mx(
+            out=a_ps1[:],
+            lhsT=slot_words[:, 128:256].bitcast(FP8X4),
+            lhsT_scale=slot_scales[:, 128:256],
+            rhs=w1_raw[:, 1 * 2 * H : 2 * 2 * H].bitcast(FP4X4),
+            rhs_scale=s1_raw[:, 1 * H : 2 * H],
+            start=True,
+            stop=True,
+        )
+        r1 = work.tile([P, PACK, P], F32, tag="r", name="r1")
+        nc.scalar.activation(out=r1[:], in_=a_ps1[:].rearrange("c (m t) -> c t m", t=PACK), func=ACT.Relu)
+        t_ps1 = psum.tile([P, PACK, C], F32, tag="t_ps", bufs=2, name="t_ps1")
         for t in range(PACK):
-            b = 3 * H + t * P
-            nc.tensor.matmul_mx(
-                out=a_ps3[:, t, :],
-                lhsT=w1_perm[:, 2 * b : 2 * b + 2 * P].bitcast(FP4X4),
-                lhsT_scale=s1_perm[:, b : b + P],
-                rhs=slot_words[:, 384:512].bitcast(FP8X4),
-                rhs_scale=slot_scales[:, 384:512],
-                start=True,
-                stop=True,
-            )
-        r3 = work.tile([P, C, PACK], F32, tag="r", name="r3")
-        nc.scalar.activation(out=r3[:], in_=a_ps3[:].rearrange("p t c -> p c t"), func=ACT.Relu)
-        y_ps1 = psum.tile([P, C], F32, tag="y_ps", name="y_ps1")
+            nc.tensor.transpose(t_ps1[:, t, :], r1[:, t, :], ident[:])
+        hb1 = work.tile([P, C, PACK], BF16, align_bytes=64, tag="hb", name="hb1")
+        nc.scalar.activation(out=hb1[:], in_=t_ps1[:].rearrange("p t c -> p c t"), func=ACT.Square)
+        h_words1 = work.tile([P, C], U32, align_bytes=64, tag="h_words", name="h_words1")
+        h_scales1 = work.tile([P, C], U8, align_bytes=64, tag="h_scales", name="h_scales1")
+        nc.vector.quantize_mx(out=h_words1[:].bitcast(FP8X4), scales=h_scales1[:], in_=hb1[:].rearrange("p c t -> p (c t)"))
+        y_ps1 = psum.tile([P, C], F32, tag="y_ps", bufs=3, name="y_ps1")
         nc.tensor.matmul_mx(
             out=y_ps1[:],
             lhsT=w2_sb[:, 1 * 2 * N : 2 * 2 * N].bitcast(FP4X4),
@@ -213,18 +189,30 @@ def tile_moe_res_mlp_relu2_kernel(
             start=True,
             stop=True,
         )
-        nc.vector.tensor_tensor(window[:].indirect(offsets[:, 0:8]), y_sb0[:], gate_sb[:, 0:128], ALU.mult)
-        hb2 = work.tile([P, C * PACK], BF16, align_bytes=64, tag="hb", name="hb2")
-        nc.scalar.activation(out=hb2[:], in_=r2[:].rearrange("p c t -> p (c t)"), func=ACT.Square)
         y_sb1 = work.tile([P, C], F32, tag="y_sb", name="y_sb1")
         nc.scalar.copy(out=y_sb1[:], in_=y_ps1[:])
+        nc.vector.tensor_tensor(window[:].indirect(offsets[:, 8:16]), y_sb1[:], gate_sb[:, 128:256], ALU.mult)
+        a_ps2 = psum.tile([P, H], F32, tag="a_ps", bufs=3, name="a_ps2")
+        nc.tensor.matmul_mx(
+            out=a_ps2[:],
+            lhsT=slot_words[:, 256:384].bitcast(FP8X4),
+            lhsT_scale=slot_scales[:, 256:384],
+            rhs=w1_raw[:, 2 * 2 * H : 3 * 2 * H].bitcast(FP4X4),
+            rhs_scale=s1_raw[:, 2 * H : 3 * H],
+            start=True,
+            stop=True,
+        )
+        r2 = work.tile([P, PACK, P], F32, tag="r", name="r2")
+        nc.vector.tensor_scalar(out=r2[:], in0=a_ps2[:].rearrange("c (m t) -> c t m", t=PACK), scalar1=0.0, scalar2=None, op0=ALU.max)
+        t_ps2 = psum.tile([P, PACK, C], F32, tag="t_ps", bufs=2, name="t_ps2")
+        for t in range(PACK):
+            nc.tensor.transpose(t_ps2[:, t, :], r2[:, t, :], ident[:])
+        hb2 = work.tile([P, C, PACK], BF16, align_bytes=64, tag="hb", name="hb2")
+        nc.scalar.activation(out=hb2[:], in_=t_ps2[:].rearrange("p t c -> p c t"), func=ACT.Square)
         h_words2 = work.tile([P, C], U32, align_bytes=64, tag="h_words", name="h_words2")
         h_scales2 = work.tile([P, C], U8, align_bytes=64, tag="h_scales", name="h_scales2")
-        nc.vector.quantize_mx(out=h_words2[:].bitcast(FP8X4), scales=h_scales2[:], in_=hb2[:])
-        nc.vector.tensor_tensor(window[:].indirect(offsets[:, 8:16]), y_sb1[:], gate_sb[:, 128:256], ALU.mult)
-        hb3 = work.tile([P, C * PACK], BF16, align_bytes=64, tag="hb", name="hb3")
-        nc.scalar.activation(out=hb3[:], in_=r3[:].rearrange("p c t -> p (c t)"), func=ACT.Square)
-        y_ps2 = psum.tile([P, C], F32, tag="y_ps", name="y_ps2")
+        nc.vector.quantize_mx(out=h_words2[:].bitcast(FP8X4), scales=h_scales2[:], in_=hb2[:].rearrange("p c t -> p (c t)"))
+        y_ps2 = psum.tile([P, C], F32, tag="y_ps", bufs=3, name="y_ps2")
         nc.tensor.matmul_mx(
             out=y_ps2[:],
             lhsT=w2_sb[:, 2 * 2 * N : 3 * 2 * N].bitcast(FP4X4),
@@ -236,11 +224,28 @@ def tile_moe_res_mlp_relu2_kernel(
         )
         y_sb2 = work.tile([P, C], F32, tag="y_sb", name="y_sb2")
         nc.scalar.copy(out=y_sb2[:], in_=y_ps2[:])
+        nc.vector.tensor_tensor(window[:].indirect(offsets[:, 16:24]), y_sb2[:], gate_sb[:, 256:384], ALU.mult)
+        a_ps3 = psum.tile([P, H], F32, tag="a_ps", bufs=3, name="a_ps3")
+        nc.tensor.matmul_mx(
+            out=a_ps3[:],
+            lhsT=slot_words[:, 384:512].bitcast(FP8X4),
+            lhsT_scale=slot_scales[:, 384:512],
+            rhs=w1_raw[:, 3 * 2 * H : 4 * 2 * H].bitcast(FP4X4),
+            rhs_scale=s1_raw[:, 3 * H : 4 * H],
+            start=True,
+            stop=True,
+        )
+        r3 = work.tile([P, PACK, P], F32, tag="r", name="r3")
+        nc.vector.tensor_scalar(out=r3[:], in0=a_ps3[:].rearrange("c (m t) -> c t m", t=PACK), scalar1=0.0, scalar2=None, op0=ALU.max)
+        t_ps3 = psum.tile([P, PACK, C], F32, tag="t_ps", bufs=2, name="t_ps3")
+        for t in range(PACK):
+            nc.tensor.transpose(t_ps3[:, t, :], r3[:, t, :], ident[:])
+        hb3 = work.tile([P, C, PACK], BF16, align_bytes=64, tag="hb", name="hb3")
+        nc.scalar.activation(out=hb3[:], in_=t_ps3[:].rearrange("p t c -> p c t"), func=ACT.Square)
         h_words3 = work.tile([P, C], U32, align_bytes=64, tag="h_words", name="h_words3")
         h_scales3 = work.tile([P, C], U8, align_bytes=64, tag="h_scales", name="h_scales3")
-        nc.vector.quantize_mx(out=h_words3[:].bitcast(FP8X4), scales=h_scales3[:], in_=hb3[:])
-        nc.vector.tensor_tensor(window[:].indirect(offsets[:, 16:24]), y_sb2[:], gate_sb[:, 256:384], ALU.mult)
-        y_ps3 = psum.tile([P, C], F32, tag="y_ps", name="y_ps3")
+        nc.vector.quantize_mx(out=h_words3[:].bitcast(FP8X4), scales=h_scales3[:], in_=hb3[:].rearrange("p c t -> p (c t)"))
+        y_ps3 = psum.tile([P, C], F32, tag="y_ps", bufs=3, name="y_ps3")
         nc.tensor.matmul_mx(
             out=y_ps3[:],
             lhsT=w2_sb[:, 3 * 2 * N : 4 * 2 * N].bitcast(FP4X4),

from contextlib import ExitStack

import concourse.mybir as mybir
from concourse.masks import make_identity

F32 = mybir.dt.float32
BF16 = mybir.dt.bfloat16
I32 = mybir.dt.int32
U32 = mybir.dt.uint32
U16 = mybir.dt.uint16
U8 = mybir.dt.uint8
FP8X4 = mybir.dt.float8_e4m3fn_x4
FP4X4 = mybir.dt.float4_e2m1fn_x4
ACT = mybir.ActivationFunctionType
ALU = mybir.AluOpType

P = 128
PACK = 4
K, T, E, C, H, N = 512, 768, 4, 128, 512, 128
S = E * C

FLOPS = 2 * S * (K * H + H * N)


def tile_moe_res_mlp_relu2_kernel(
    tc, xT, xr, w1_words, w1_scales, w2_words, w2_scales, gate, offs, out
):
    nc = tc.nc
    with ExitStack() as ctx:
        keep = ctx.enter_context(tc.tile_pool(name="keep", bufs=1))
        work = ctx.enter_context(tc.tile_pool(name="work", bufs=4))
        psum = ctx.enter_context(tc.psum_pool(name="psum", bufs=1))

        offsets = keep.tile([P, S // 16], U16, name="offsets")
        w1_raw = keep.tile([P, E * 2 * H], U8, align_bytes=64, name="w1_raw")
        s1_raw = keep.tile([P, E * H], U8, align_bytes=64, name="s1_raw")
        w1_perm = keep.tile([P, 1 * 2 * H], U8, align_bytes=64, name="w1_perm")
        s1_perm = keep.tile([P, 1 * H], U8, align_bytes=64, name="s1_perm")
        w2_sb = keep.tile([P, E * 2 * N], U8, align_bytes=64, name="w2_sb")
        s2_sb = keep.tile([P, E * N], U8, align_bytes=64, name="s2_sb")
        tok_words = keep.tile([P, T], U32, align_bytes=64, name="tok_words")
        tok_scales = keep.tile([P, T], U8, align_bytes=64, name="tok_scales")
        slot_words = keep.tile([P, S], U32, align_bytes=64, name="slot_words")
        slot_scales = keep.tile([P, S], U8, align_bytes=64, name="slot_scales")
        window = keep.tile([P, T], F32, name="window")
        xr_sb = keep.tile([P, T], F32, name="xr_sb")
        gate_sb = keep.tile([P, S], F32, name="gate_sb")
        out_sb = keep.tile([P, T], F32, name="out_sb")
        ident = keep.tile([P, P], F32, name="ident")
        dummy = keep.tile([P, 2], F32, name="dummy")

        nc.gpsimd.memset(s1_raw[:].bitcast(I32), 0)
        nc.gpsimd.memset(dummy[:, 0:1], 0.0)
        nc.gpsimd.memset(s2_sb[:].bitcast(I32), 0)
        nc.gpsimd.memset(tok_scales[:], 0)
        make_identity(nc, ident[:])
        nc.gpsimd.memset(window[:], 0.0)
        nc.scalar.activation(out=dummy[:, 1:2], in_=dummy[:, 0:1], func=ACT.Relu)
        nc.sync.dma_start(
            out=w1_raw[:].bitcast(I32).rearrange("p (e b) -> p e b", e=E)[:, 0:1, :],
            in_=w1_words.bitcast(I32).rearrange("e s p b -> p (e s) b")[:, 0:1, :],
        )
        raw0 = keep.tile([P, PACK, 256], F32, name="raw0")
        nc.sync.dma_start(out=raw0[:], in_=xT.rearrange("(p j) t -> p j t", j=PACK)[:, :, 0:256])
        for q in range(4):
            nc.sync.dma_start(
                out=s1_raw[32 * q : 32 * q + 4, :].bitcast(I32).rearrange("r (e b) -> r e b", e=E),
                in_=w1_scales.bitcast(I32).rearrange("e s r b -> r (e s) b")[4 * q : 4 * q + 4, :, :],
            )
        raw1 = keep.tile([P, PACK, 256], F32, name="raw1")
        nc.sync.dma_start(out=raw1[:], in_=xT.rearrange("(p j) t -> p j t", j=PACK)[:, :, 256:512])
        nc.sync.dma_start(offsets[:], offs)
        raw2 = keep.tile([P, PACK, 256], F32, name="raw2")
        nc.sync.dma_start(out=raw2[:], in_=xT.rearrange("(p j) t -> p j t", j=PACK)[:, :, 512:768])
        nc.sync.dma_start(
            out=w1_raw[:].bitcast(I32).rearrange("p (e b) -> p e b", e=E)[:, 1:4, :],
            in_=w1_words.bitcast(I32).rearrange("e s p b -> p (e s) b")[:, 1:4, :],
        )
        nc.sync.dma_start(
            out=w2_sb[:].bitcast(I32).rearrange("p (e b) -> p e b", e=E),
            in_=w2_words.bitcast(I32).rearrange("e s p b -> p (e s) b"),
        )
        for q in range(4):
            nc.sync.dma_start(
                out=s2_sb[32 * q : 32 * q + 4, :].bitcast(I32).rearrange("r (e b) -> r e b", e=E),
                in_=w2_scales.bitcast(I32).rearrange("e s r b -> r (e s) b")[4 * q : 4 * q + 4, :, :],
            )
        nc.sync.dma_start(out=gate_sb[:], in_=gate)
        nc.sync.dma_start(out=xr_sb[:], in_=xr)
        nc.vector.tensor_copy(
            out=w1_perm[:].bitcast(U16)[:, 0 * H : 1 * H].rearrange("p (t m) -> p t m", t=PACK),
            in_=w1_raw[:].bitcast(U16)[:, 0 * H : 1 * H].rearrange("p (m t) -> p t m", t=PACK),
        )
        nc.vector.tensor_copy(
            out=s1_perm[:, 0 * H : 1 * H].rearrange("p (t m) -> p t m", t=PACK),
            in_=s1_raw[:, 0 * H : 1 * H].rearrange("p (m t) -> p t m", t=PACK),
        )
        grouped0 = keep.tile([P, 256, PACK], BF16, align_bytes=64, name="grouped0")
        nc.scalar.copy(out=grouped0[:, 0:160, :].rearrange("p (c i) j -> p c j i", i=4), in_=raw0[:, :, 0:160].rearrange("p j (c i) -> p c j i", i=4))
        nc.vector.tensor_copy(out=grouped0[:, 160:256, :].rearrange("p (c i) j -> p c j i", i=4), in_=raw0[:, :, 160:256].rearrange("p j (c i) -> p c j i", i=4))
        nc.vector.quantize_mx(
            out=tok_words[:, 0:256].bitcast(FP8X4),
            scales=tok_scales[:, 0:256],
            in_=grouped0[:, 0:256, :].rearrange("p t j -> p (t j)"),
        )
        grouped1 = keep.tile([P, 256, PACK], BF16, align_bytes=64, name="grouped1")
        nc.scalar.copy(out=grouped1[:, 0:144, :].rearrange("p (c i) j -> p c j i", i=4), in_=raw1[:, :, 0:144].rearrange("p j (c i) -> p c j i", i=4))
        nc.vector.tensor_copy(out=grouped1[:, 144:256, :].rearrange("p (c i) j -> p c j i", i=4), in_=raw1[:, :, 144:256].rearrange("p j (c i) -> p c j i", i=4))
        nc.vector.quantize_mx(
            out=tok_words[:, 256:512].bitcast(FP8X4),
            scales=tok_scales[:, 256:512],
            in_=grouped1[:, 0:256, :].rearrange("p t j -> p (t j)"),
        )
        grouped2 = keep.tile([P, 256, PACK], BF16, align_bytes=64, name="grouped2")
        nc.scalar.copy(out=grouped2[:, 0:80, :].rearrange("p (c i) j -> p c j i", i=4), in_=raw2[:, :, 0:80].rearrange("p j (c i) -> p c j i", i=4))
        nc.vector.tensor_copy(out=grouped2[:, 80:256, :].rearrange("p (c i) j -> p c j i", i=4), in_=raw2[:, :, 80:256].rearrange("p j (c i) -> p c j i", i=4))
        nc.vector.quantize_mx(
            out=tok_words[:, 512:768].bitcast(FP8X4),
            scales=tok_scales[:, 512:768],
            in_=grouped2[:, 0:256, :].rearrange("p t j -> p (t j)"),
        )
        nc.vector.tensor_copy(out=slot_words[:, 0:128], in_=tok_words[:].indirect(offsets[:, 0:8]))
        nc.vector.tensor_copy(out=slot_scales[:, 0:128], in_=tok_scales[:].indirect(offsets[:, 0:8]))
        nc.vector.tensor_copy(out=slot_words[:, 128:256], in_=tok_words[:].indirect(offsets[:, 8:16]))
        nc.vector.tensor_copy(out=slot_scales[:, 128:256], in_=tok_scales[:].indirect(offsets[:, 8:16]))
        nc.vector.tensor_copy(out=slot_words[:, 256:384], in_=tok_words[:].indirect(offsets[:, 16:24]))
        nc.vector.tensor_copy(out=slot_scales[:, 256:384], in_=tok_scales[:].indirect(offsets[:, 16:24]))
        nc.vector.tensor_copy(out=slot_words[:, 384:512], in_=tok_words[:].indirect(offsets[:, 24:32]))
        nc.vector.tensor_copy(out=slot_scales[:, 384:512], in_=tok_scales[:].indirect(offsets[:, 24:32]))
        a_ps0 = psum.tile([P, PACK, C], F32, tag="a_ps", bufs=3, name="a_ps0")
        for t in range(PACK):
            b = 0 * H + t * P
            nc.tensor.matmul_mx(
                out=a_ps0[:, t, :],
                lhsT=w1_perm[:, 2 * b : 2 * b + 2 * P].bitcast(FP4X4),
                lhsT_scale=s1_perm[:, b : b + P],
                rhs=slot_words[:, 0:128].bitcast(FP8X4),
                rhs_scale=slot_scales[:, 0:128],
                start=True,
                stop=True,
            )
        r0 = work.tile([P, C, PACK], F32, tag="r", name="r0")
        nc.scalar.activation(out=r0[:], in_=a_ps0[:].rearrange("p t c -> p c t"), func=ACT.Relu)
        hb0 = work.tile([P, C, PACK], BF16, align_bytes=64, tag="hb", name="hb0")
        nc.scalar.activation(out=hb0[:], in_=r0[:], func=ACT.Square)
        h_words0 = work.tile([P, C], U32, align_bytes=64, tag="h_words", name="h_words0")
        h_scales0 = work.tile([P, C], U8, align_bytes=64, tag="h_scales", name="h_scales0")
        nc.vector.quantize_mx(out=h_words0[:].bitcast(FP8X4), scales=h_scales0[:], in_=hb0[:].rearrange("p c t -> p (c t)"))
        y_ps0 = psum.tile([P, C], F32, tag="y_ps", bufs=3, name="y_ps0")
        nc.tensor.matmul_mx(
            out=y_ps0[:],
            lhsT=w2_sb[:, 0 * 2 * N : 1 * 2 * N].bitcast(FP4X4),
            lhsT_scale=s2_sb[:, 0 * N : 1 * N],
            rhs=h_words0[:].bitcast(FP8X4),
            rhs_scale=h_scales0[:],
            start=True,
            stop=True,
        )
        y_sb0 = work.tile([P, C], F32, tag="y_sb", name="y_sb0")
        nc.scalar.copy(out=y_sb0[:], in_=y_ps0[:])
        nc.vector.tensor_tensor(window[:].indirect(offsets[:, 0:8]), y_sb0[:], gate_sb[:, 0:128], ALU.mult)
        a_ps1 = psum.tile([P, H], F32, tag="a_ps", bufs=3, name="a_ps1")
        nc.tensor.matmul_mx(
            out=a_ps1[:],
            lhsT=slot_words[:, 128:256].bitcast(FP8X4),
            lhsT_scale=slot_scales[:, 128:256],
            rhs=w1_raw[:, 1 * 2 * H : 2 * 2 * H].bitcast(FP4X4),
            rhs_scale=s1_raw[:, 1 * H : 2 * H],
            start=True,
            stop=True,
        )
        r1 = work.tile([P, PACK, P], F32, tag="r", name="r1")
        nc.scalar.activation(out=r1[:], in_=a_ps1[:].rearrange("c (m t) -> c t m", t=PACK), func=ACT.Relu)
        t_ps1 = psum.tile([P, PACK, C], F32, tag="t_ps", bufs=2, name="t_ps1")
        for t in range(PACK):
            nc.tensor.transpose(t_ps1[:, t, :], r1[:, t, :], ident[:])
        hb1 = work.tile([P, C, PACK], BF16, align_bytes=64, tag="hb", name="hb1")
        nc.scalar.activation(out=hb1[:], in_=t_ps1[:].rearrange("p t c -> p c t"), func=ACT.Square)
        h_words1 = work.tile([P, C], U32, align_bytes=64, tag="h_words", name="h_words1")
        h_scales1 = work.tile([P, C], U8, align_bytes=64, tag="h_scales", name="h_scales1")
        nc.vector.quantize_mx(out=h_words1[:].bitcast(FP8X4), scales=h_scales1[:], in_=hb1[:].rearrange("p c t -> p (c t)"))
        y_ps1 = psum.tile([P, C], F32, tag="y_ps", bufs=3, name="y_ps1")
        nc.tensor.matmul_mx(
            out=y_ps1[:],
            lhsT=w2_sb[:, 1 * 2 * N : 2 * 2 * N].bitcast(FP4X4),
            lhsT_scale=s2_sb[:, 1 * N : 2 * N],
            rhs=h_words1[:].bitcast(FP8X4),
            rhs_scale=h_scales1[:],
            start=True,
            stop=True,
        )
        y_sb1 = work.tile([P, C], F32, tag="y_sb", name="y_sb1")
        nc.scalar.copy(out=y_sb1[:], in_=y_ps1[:])
        nc.vector.tensor_tensor(window[:].indirect(offsets[:, 8:16]), y_sb1[:], gate_sb[:, 128:256], ALU.mult)
        a_ps2 = psum.tile([P, H], F32, tag="a_ps", bufs=3, name="a_ps2")
        nc.tensor.matmul_mx(
            out=a_ps2[:],
            lhsT=slot_words[:, 256:384].bitcast(FP8X4),
            lhsT_scale=slot_scales[:, 256:384],
            rhs=w1_raw[:, 2 * 2 * H : 3 * 2 * H].bitcast(FP4X4),
            rhs_scale=s1_raw[:, 2 * H : 3 * H],
            start=True,
            stop=True,
        )
        r2 = work.tile([P, PACK, P], F32, tag="r", name="r2")
        nc.vector.tensor_scalar(out=r2[:], in0=a_ps2[:].rearrange("c (m t) -> c t m", t=PACK), scalar1=0.0, scalar2=None, op0=ALU.max)
        t_ps2 = psum.tile([P, PACK, C], F32, tag="t_ps", bufs=2, name="t_ps2")
        for t in range(PACK):
            nc.tensor.transpose(t_ps2[:, t, :], r2[:, t, :], ident[:])
        hb2 = work.tile([P, C, PACK], BF16, align_bytes=64, tag="hb", name="hb2")
        nc.scalar.activation(out=hb2[:], in_=t_ps2[:].rearrange("p t c -> p c t"), func=ACT.Square)
        h_words2 = work.tile([P, C], U32, align_bytes=64, tag="h_words", name="h_words2")
        h_scales2 = work.tile([P, C], U8, align_bytes=64, tag="h_scales", name="h_scales2")
        nc.vector.quantize_mx(out=h_words2[:].bitcast(FP8X4), scales=h_scales2[:], in_=hb2[:].rearrange("p c t -> p (c t)"))
        y_ps2 = psum.tile([P, C], F32, tag="y_ps", bufs=3, name="y_ps2")
        nc.tensor.matmul_mx(
            out=y_ps2[:],
            lhsT=w2_sb[:, 2 * 2 * N : 3 * 2 * N].bitcast(FP4X4),
            lhsT_scale=s2_sb[:, 2 * N : 3 * N],
            rhs=h_words2[:].bitcast(FP8X4),
            rhs_scale=h_scales2[:],
            start=True,
            stop=True,
        )
        y_sb2 = work.tile([P, C], F32, tag="y_sb", name="y_sb2")
        nc.scalar.copy(out=y_sb2[:], in_=y_ps2[:])
        nc.vector.tensor_tensor(window[:].indirect(offsets[:, 16:24]), y_sb2[:], gate_sb[:, 256:384], ALU.mult)
        a_ps3 = psum.tile([P, H], F32, tag="a_ps", bufs=3, name="a_ps3")
        nc.tensor.matmul_mx(
            out=a_ps3[:],
            lhsT=slot_words[:, 384:512].bitcast(FP8X4),
            lhsT_scale=slot_scales[:, 384:512],
            rhs=w1_raw[:, 3 * 2 * H : 4 * 2 * H].bitcast(FP4X4),
            rhs_scale=s1_raw[:, 3 * H : 4 * H],
            start=True,
            stop=True,
        )
        r3 = work.tile([P, PACK, P], F32, tag="r", name="r3")
        nc.vector.tensor_scalar(out=r3[:], in0=a_ps3[:].rearrange("c (m t) -> c t m", t=PACK), scalar1=0.0, scalar2=None, op0=ALU.max)
        t_ps3 = psum.tile([P, PACK, C], F32, tag="t_ps", bufs=2, name="t_ps3")
        for t in range(PACK):
            nc.tensor.transpose(t_ps3[:, t, :], r3[:, t, :], ident[:])
        hb3 = work.tile([P, C, PACK], BF16, align_bytes=64, tag="hb", name="hb3")
        nc.scalar.activation(out=hb3[:], in_=t_ps3[:].rearrange("p t c -> p c t"), func=ACT.Square)
        h_words3 = work.tile([P, C], U32, align_bytes=64, tag="h_words", name="h_words3")
        h_scales3 = work.tile([P, C], U8, align_bytes=64, tag="h_scales", name="h_scales3")
        nc.vector.quantize_mx(out=h_words3[:].bitcast(FP8X4), scales=h_scales3[:], in_=hb3[:].rearrange("p c t -> p (c t)"))
        y_ps3 = psum.tile([P, C], F32, tag="y_ps", bufs=3, name="y_ps3")
        nc.tensor.matmul_mx(
            out=y_ps3[:],
            lhsT=w2_sb[:, 3 * 2 * N : 4 * 2 * N].bitcast(FP4X4),
            lhsT_scale=s2_sb[:, 3 * N : 4 * N],
            rhs=h_words3[:].bitcast(FP8X4),
            rhs_scale=h_scales3[:],
            start=True,
            stop=True,
        )
        y_sb3 = work.tile([P, C], F32, tag="y_sb", name="y_sb3")
        nc.scalar.copy(out=y_sb3[:], in_=y_ps3[:])
        nc.vector.tensor_tensor(window[:].indirect(offsets[:, 24:32]), y_sb3[:], gate_sb[:, 384:512], ALU.mult)
        nc.vector.tensor_tensor(out_sb[:, 0:384], window[:, 0:384], xr_sb[:, 0:384], ALU.add)
        nc.sync.dma_start(out=out[:, 0:384], in_=out_sb[:, 0:384])
        nc.vector.tensor_tensor(out_sb[:, 384:768], window[:, 384:768], xr_sb[:, 384:768], ALU.add)
        nc.sync.dma_start(out=out[:, 384:768], in_=out_sb[:, 384:768])
